import numpy as np
CORES = [50,106,114,52,108,116]
N = 6
def setup_inputs(rng):
    m = (rng.standard_normal((N, 128, 128), dtype=np.float32) / 11)
    return {"m": m, "mt": m.transpose(0, 2, 1).copy()}
def setup_inputs_low(rng):
    d = setup_inputs(rng)
    for k in ("m", "mt"): d[k] = (d[k].astype(np.float32) * 0.125).astype(d[k].dtype)
    return d
def reference(m, mt):
    M = m.astype(np.float64); p = M[0]
    for r in range(1, N):
        p = p @ M[r]
    p = p.astype(np.float32)
    return {"y": np.broadcast_to(p, (N, 128, 128))}

@@ -1,0 +1,147 @@
+from concourse.bass import DstId, RemoteDMATransfer
+
+_F = "float32"
+_SB = ["s_a0", "s_m1", "s_a2", "s_m3", "s_a4", "s_m5", "s_ut", "s_v", "s_qt", "s_r", "s_p"]
+SCRATCH = {
+    "d_stage": ("dram", [128, 128], _F),
+    "d_m4": ("dram", [128, 128], _F),
+}
+for _n in _SB:
+    SCRATCH[_n] = ("sbuf", [128, 128], _F)
+for _n in ["p_v", "p_u", "p_q", "p_r", "p_p"]:
+    SCRATCH[_n] = ("psum", [128, 512], _F)
+
+SEMAPHORES = ["ld", "ld2", "a0", "m1", "a2", "m3", "d4", "a4", "m5", "qt", "snt",
+              "mmv", "mmu", "mmq", "mmr", "mmp", "cpv", "cpu", "cpq", "cpr", "cpp", "st"]
+
+
+def _engines(mask):
+    return [b for b in range(mask.bit_length()) if (mask >> b) & 1]
+
+
+def _as_mask(bits):
+    m = 0
+    for b in bits:
+        m |= 1 << b
+    return m
+
+
+def _count(mask):
+    return len(_engines(mask))
+
+
+def rank_program(g, core, T, topo):
+    r = T.rank_of(core)
+    if r is None:
+        return
+    c = T.cores
+    S = T.sem
+    te, ve, sy, sc = g.tensor, g.vector, g.sync, g.scalar
+
+    near = [d for d in c if d != core and topo.chip(d) == topo.chip(core)]
+    far = [d for d in c if topo.chip(d) != topo.chip(core)]
+    on_eng = _engines(topo.mask(core, near[0]))
+    off_eng = _engines(topo.mask(core, far[0]))
+    LOW = _as_mask(off_eng)
+    HIGH = _as_mask([e for e in on_eng if e not in off_eng])
+    THIN = _as_mask(on_eng[::4])
+    nl, nh, nt = _count(LOW), _count(HIGH), _count(THIN)
+    sent = [0]
+
+    def xfer(dsts, mask, src, dst, sem):
+        for d in dsts:
+            if not topo.may_write(core, d) or (mask & ~topo.mask(core, d)):
+                raise ValueError("core %d cannot write so to core %d" % (core, d))
+        ids = [DstId(rid=topo.addr(d)[0], pnc=topo.addr(d)[1]) for d in dsts]
+        sent[0] += _count(mask)
+        return RemoteDMATransfer(dst_ids=ids, dma_engine_mask=mask, remote_sem=sem,
+                                 srcs=[src], dsts=[dst for _ in dsts])
+
+    def call(*transfers):
+        g.remote_dma_fused(list(transfers), local_sem=S.snt)
+
+    def mm(out, lhsT, rhs, sem):
+        te.matmul(out[:, 0:128], lhsT[:], rhs[:], True, True).then_inc(sem, 1)
+
+    def evac(psum, sbuf, after, sem):
+        ve.wait_ge(after, 1)
+        ve.tensor_copy(sbuf[:], psum[:, 0:128]).then_inc(sem, 1)
+
+    def stage(inp, own=None):
+        sy.dma_start(T.d_stage[:], inp[:]).then_inc(S.ld, 16)
+        if own is not None:
+            sc.wait_ge(S.ld, 16)
+            sc.dma_start(own[:], inp[:]).then_inc(S.ld2, 16)
+        g.wait_ge(S.ld, 16)
+
+    def head(a0_ready, a2_ready):
+        te.wait_ge(*a2_ready)
+        te.wait_ge(S.m3, nl)
+        mm(T.p_v, T.s_a2, T.s_m3, S.mmv)
+        evac(T.p_v, T.s_v, S.mmv, S.cpv)
+        te.wait_ge(*a0_ready)
+        te.wait_ge(S.m1, nl)
+        mm(T.p_u, T.s_m1, T.s_a0, S.mmu)
+        evac(T.p_u, T.s_ut, S.mmu, S.cpu)
+        te.wait_ge(S.cpv, 1)
+        te.wait_ge(S.cpu, 1)
+        mm(T.p_q, T.s_v, T.s_ut, S.mmq)
+        evac(T.p_q, T.s_qt, S.mmq, S.cpq)
+
+    def tail(a4_ready, m5_ready, qt_ready):
+        te.wait_ge(*a4_ready)
+        te.wait_ge(*m5_ready)
+        mm(T.p_r, T.s_a4, T.s_m5, S.mmr)
+        evac(T.p_r, T.s_r, S.mmr, S.cpr)
+        te.wait_ge(S.cpr, 1)
+        te.wait_ge(*qt_ready)
+        mm(T.p_p, T.s_qt, T.s_r, S.mmp)
+        evac(T.p_p, T.s_p, S.mmp, S.cpp)
+        sy.wait_ge(S.cpp, 1)
+        sy.dma_start(T.y[:], T.s_p[:]).then_inc(S.st, 16)
+        sy.wait_ge(S.st, 16)
+
+    st = T.d_stage[:]
+    if r == 0:
+        stage(T.mt, T.s_a0)
+        call(xfer([c[2]], LOW, st, T.s_a0[:], S.a0))
+        head((S.ld2, 16), (S.a2, nl))
+        g.wait_ge(S.m5, nl)
+        call(xfer([c[1]], LOW, T.s_m5[:], T.s_m5[:], S.m5), xfer([c[3]], HIGH, T.s_m5[:], T.s_m5[:], S.m5))
+        g.wait_ge(S.cpq, 1)
+        call(xfer([c[1]], LOW, T.s_qt[:], T.s_qt[:], S.qt), xfer([c[3]], HIGH, T.s_qt[:], T.s_qt[:], S.qt))
+        tail((S.a4, nl), (S.m5, nl), (S.cpq, 1))
+    elif r == 2:
+        stage(T.mt, T.s_a2)
+        call(xfer([c[0]], LOW, st, T.s_a2[:], S.a2))
+        head((S.a0, nl), (S.ld2, 16))
+        g.wait_ge(S.m5, nh)
+        call(xfer([c[4]], LOW, T.s_m5[:], T.s_m5[:], S.m5))
+        g.wait_ge(S.cpq, 1)
+        call(xfer([c[4]], LOW, T.s_qt[:], T.s_qt[:], S.qt))
+        call(xfer([c[5]], LOW, T.s_qt[:], T.s_qt[:], S.qt))
+        tail((S.a4, nl), (S.m5, nh), (S.cpq, 1))
+    elif r == 1:
+        stage(T.m)
+        call(xfer([c[2]], LOW, st, T.s_m1[:], S.m1))
+        call(xfer([c[0]], LOW, st, T.s_m1[:], S.m1))
+        g.wait_ge(S.d4, nt)
+        call(xfer([c[2], c[0], c[5], c[3]], LOW, T.d_m4[:], T.s_a4[:], S.a4))
+        sc.wait_ge(S.d4, nt)
+        sc.dma_start(T.s_a4[:], T.d_m4[:]).then_inc(S.ld2, 16)
+        tail((S.ld2, 16), (S.m5, nl), (S.qt, nl))
+    elif r == 3:
+        stage(T.m)
+        call(xfer([c[2]], LOW, st, T.s_m3[:], S.m3))
+        call(xfer([c[0]], HIGH, st, T.s_m3[:], S.m3))
+        tail((S.a4, nl), (S.m5, nh), (S.qt, nh))
+    elif r == 4:
+        stage(T.mt, T.s_a4)
+        call(xfer([c[1]], THIN, st, T.d_m4[:], S.d4))
+        tail((S.ld2, 16), (S.m5, nl), (S.qt, nl))
+    else:
+        stage(T.m, T.s_m5)
+        call(xfer([c[0]], LOW, st, T.s_m5[:], S.m5))
+        call(xfer([c[2]], HIGH, st, T.s_m5[:], S.m5))
+        tail((S.a4, nl), (S.ld2, 16), (S.qt, nl))
+    g.wait_ge(S.snt, sent[0])

@@ -1,18 +1,23 @@
 from concourse.bass import DstId, RemoteDMATransfer
 
+M4_PLAN = [[2, 0], [5], [3]]
+M5_PLAN = [[1], [4]]
+
 _F = "float32"
 _SB = ["s_a0", "s_m1", "s_a2", "s_m3", "s_a4", "s_m5", "s_ut", "s_v", "s_qt", "s_r", "s_p"]
 SCRATCH = {
     "d_stage": ("dram", [128, 128], _F),
-    "d_m4": ("dram", [128, 128], _F),
+    "d_in": ("dram", [128, 128], _F),
 }
 for _n in _SB:
     SCRATCH[_n] = ("sbuf", [128, 128], _F)
-for _n in ["p_v", "p_u", "p_q", "p_r", "p_p"]:
-    SCRATCH[_n] = ("psum", [128, 512], _F)
+for _k in range(8):
+    SCRATCH["b%d" % _k] = ("psum", [128, 512], _F)
 
-SEMAPHORES = ["ld", "ld2", "a0", "m1", "a2", "m3", "d4", "a4", "m5", "qt", "snt",
-              "mmv", "mmu", "mmq", "mmr", "mmp", "cpv", "cpu", "cpq", "cpr", "cpp", "st"]
+SEMAPHORES = ["ld", "ld2", "ld3", "a0", "m1", "a2", "m3", "din", "a4", "m5", "vv", "qt", "snt", "st"]
+for _n in "vuqrp":
+    for _k in range(2):
+        SEMAPHORES += ["mm%s%d" % (_n, _k), "cp%s%d" % (_n, _k)]
 
 
 def _engines(mask):
@@ -32,9 +37,17 @@ def _count(mask):
 
 def rank_program(g, core, T, topo):
     r = T.rank_of(core)
-    if r is None:
-        return
     c = T.cores
+
+    def outside(owner, target):
+        return [x for x in range(topo.CORES_PER_CHIP * topo.CHIPS)
+                if x not in c and topo.chip(x) == topo.chip(owner) and topo.die(x) == topo.die(owner)
+                and topo.may_write(x, target)]
+
+    carriers4 = [c[1]] + outside(c[4], c[3])[:len(M4_PLAN) - 1]
+    carriers5 = outside(c[5], c[1])[:len(M5_PLAN)]
+    if core not in c and core not in carriers4 and core not in carriers5:
+        return
     S = T.sem
     te, ve, sy, sc = g.tensor, g.vector, g.sync, g.scalar
 
@@ -44,8 +57,8 @@ def rank_program(g, core, T, topo):
     off_eng = _engines(topo.mask(core, far[0]))
     LOW = _as_mask(off_eng)
     HIGH = _as_mask([e for e in on_eng if e not in off_eng])
-    THIN = _as_mask(on_eng[::4])
-    nl, nh, nt = _count(LOW), _count(HIGH), _count(THIN)
+    THIN = [_as_mask(on_eng[k::4]) for k in (0, 2, 1, 3)]
+    nl, nh, nt = _count(LOW), _count(HIGH), _count(THIN[0])
     sent = [0]
 
     def xfer(dsts, mask, src, dst, sem):
@@ -60,12 +73,23 @@ def rank_program(g, core, T, topo):
     def call(*transfers):
         g.remote_dma_fused(list(transfers), local_sem=S.snt)
 
-    def mm(out, lhsT, rhs, sem):
-        te.matmul(out[:, 0:128], lhsT[:], rhs[:], True, True).then_inc(sem, 1)
+    def product(name, lhsT, rhs, out, banks, ready, ready_half=None):
+        for w in ready:
+            te.wait_ge(*w)
+        for h in range(2):
+            cols = slice(64 * h, 64 * h + 64)
+            if ready_half is not None:
+                te.wait_ge(S["cp%s%d" % (ready_half, h)], 1)
+            te.matmul(T[banks[h]][:, 0:64], lhsT[:], rhs[:, cols], True, True).then_inc(S["mm%s%d" % (name, h)], 1)
+            ve.wait_ge(S["mm%s%d" % (name, h)], 1)
+            ve.tensor_copy(out[:, cols], T[banks[h]][:, 0:64]).then_inc(S["cp%s%d" % (name, h)], 1)
 
-    def evac(psum, sbuf, after, sem):
-        ve.wait_ge(after, 1)
-        ve.tensor_copy(sbuf[:], psum[:, 0:128]).then_inc(sem, 1)
+    def done(name):
+        return [(S["cp%s%d" % (name, h)], 1) for h in range(2)]
+
+    def g_wait(waits):
+        for w in waits:
+            g.wait_ge(*w)
 
     def stage(inp, own=None):
         sy.dma_start(T.d_stage[:], inp[:]).then_inc(S.ld, 16)
@@ -74,74 +98,91 @@ def rank_program(g, core, T, topo):
             sc.dma_start(own[:], inp[:]).then_inc(S.ld2, 16)
         g.wait_ge(S.ld, 16)
 
-    def head(a0_ready, a2_ready):
-        te.wait_ge(*a2_ready)
-        te.wait_ge(S.m3, nl)
-        mm(T.p_v, T.s_a2, T.s_m3, S.mmv)
-        evac(T.p_v, T.s_v, S.mmv, S.cpv)
-        te.wait_ge(*a0_ready)
-        te.wait_ge(S.m1, nl)
-        mm(T.p_u, T.s_m1, T.s_a0, S.mmu)
-        evac(T.p_u, T.s_ut, S.mmu, S.cpu)
-        te.wait_ge(S.cpv, 1)
-        te.wait_ge(S.cpu, 1)
-        mm(T.p_q, T.s_v, T.s_ut, S.mmq)
-        evac(T.p_q, T.s_qt, S.mmq, S.cpq)
+    def carry(ranks, dst, sem):
+        g.wait_ge(S.din, nt)
+        call(xfer([c[k] for k in ranks], LOW, T.d_in[:], dst[:], sem))
 
-    def tail(a4_ready, m5_ready, qt_ready):
-        te.wait_ge(*a4_ready)
-        te.wait_ge(*m5_ready)
-        mm(T.p_r, T.s_a4, T.s_m5, S.mmr)
-        evac(T.p_r, T.s_r, S.mmr, S.cpr)
-        te.wait_ge(S.cpr, 1)
-        te.wait_ge(*qt_ready)
-        mm(T.p_p, T.s_qt, T.s_r, S.mmp)
-        evac(T.p_p, T.s_p, S.mmp, S.cpp)
-        sy.wait_ge(S.cpp, 1)
+    def make_v(a2_ready, m3_ready):
+        product("v", T.s_a2, T.s_m3, T.s_v, ("b0", "b7"), [a2_ready, m3_ready])
+
+    def make_u(a0_ready, m1_ready):
+        product("u", T.s_m1, T.s_a0, T.s_ut, ("b1", "b2"), [a0_ready, m1_ready])
+
+    def make_q(v_ready):
+        product("q", T.s_v, T.s_ut, T.s_qt, ("b3", "b4"), v_ready, "u")
+
+    def make_r(a4_ready, m5_ready):
+        product("r", T.s_a4, T.s_m5, T.s_r, ("b5", "b6"), [a4_ready, m5_ready])
+
+    def make_p(qt_ready):
+        product("p", T.s_qt, T.s_r, T.s_p, ("b0", "b7"), qt_ready, "r")
+        for w in done("p"):
+            sy.wait_ge(*w)
         sy.dma_start(T.y[:], T.s_p[:]).then_inc(S.st, 16)
         sy.wait_ge(S.st, 16)
 
     st = T.d_stage[:]
-    if r == 0:
+    if core in carriers5:
+        carry(M5_PLAN[carriers5.index(core)], T.s_m5, S.m5)
+    elif r is None:
+        carry(M4_PLAN[carriers4.index(core)], T.s_a4, S.a4)
+    elif r == 0:
         stage(T.mt, T.s_a0)
         call(xfer([c[2]], LOW, st, T.s_a0[:], S.a0))
-        head((S.ld2, 16), (S.a2, nl))
-        g.wait_ge(S.m5, nl)
-        call(xfer([c[1]], LOW, T.s_m5[:], T.s_m5[:], S.m5), xfer([c[3]], HIGH, T.s_m5[:], T.s_m5[:], S.m5))
-        g.wait_ge(S.cpq, 1)
-        call(xfer([c[1]], LOW, T.s_qt[:], T.s_qt[:], S.qt), xfer([c[3]], HIGH, T.s_qt[:], T.s_qt[:], S.qt))
-        tail((S.a4, nl), (S.m5, nl), (S.cpq, 1))
+        call(xfer([c[1], c[4]], LOW, st, T.s_a0[:], S.a0), xfer([c[3]], HIGH, st, T.s_a0[:], S.a0))
+        g_wait(done("v"))
+        call(xfer([c[1]], LOW, T.s_v[:], T.s_v[:], S.vv))
+        make_v((S.a2, nl), (S.m3, nh))
+        make_u((S.ld2, 16), (S.m1, nl))
+        make_q(done("v"))
+        make_r((S.a4, nl), (S.m5, nl))
+        make_p(done("q"))
     elif r == 2:
         stage(T.mt, T.s_a2)
         call(xfer([c[0]], LOW, st, T.s_a2[:], S.a2))
-        head((S.a0, nl), (S.ld2, 16))
-        g.wait_ge(S.m5, nh)
-        call(xfer([c[4]], LOW, T.s_m5[:], T.s_m5[:], S.m5))
-        g.wait_ge(S.cpq, 1)
-        call(xfer([c[4]], LOW, T.s_qt[:], T.s_qt[:], S.qt))
+        call(xfer([c[3]], LOW, st, T.s_a2[:], S.a2))
+        g_wait(done("v"))
+        call(xfer([c[4]], LOW, T.s_v[:], T.s_v[:], S.vv))
+        g_wait(done("q"))
         call(xfer([c[5]], LOW, T.s_qt[:], T.s_qt[:], S.qt))
-        tail((S.a4, nl), (S.m5, nh), (S.cpq, 1))
-    elif r == 1:
-        stage(T.m)
-        call(xfer([c[2]], LOW, st, T.s_m1[:], S.m1))
-        call(xfer([c[0]], LOW, st, T.s_m1[:], S.m1))
-        g.wait_ge(S.d4, nt)
-        call(xfer([c[2], c[0], c[5], c[3]], LOW, T.d_m4[:], T.s_a4[:], S.a4))
-        sc.wait_ge(S.d4, nt)
-        sc.dma_start(T.s_a4[:], T.d_m4[:]).then_inc(S.ld2, 16)
-        tail((S.ld2, 16), (S.m5, nl), (S.qt, nl))
+        make_v((S.ld2, 16), (S.m3, nl))
+        make_u((S.a0, nl), (S.m1, nl))
+        make_q(done("v"))
+        make_r((S.a4, nl), (S.m5, nh))
+        make_p(done("q"))
     elif r == 3:
-        stage(T.m)
+        stage(T.m, T.s_m3)
         call(xfer([c[2]], LOW, st, T.s_m3[:], S.m3))
         call(xfer([c[0]], HIGH, st, T.s_m3[:], S.m3))
-        tail((S.a4, nl), (S.m5, nh), (S.qt, nh))
+        make_v((S.a2, nl), (S.ld2, 16))
+        make_u((S.a0, nh), (S.m1, nl))
+        make_q(done("v"))
+        make_r((S.a4, nl), (S.m5, nl))
+        make_p(done("q"))
+    elif r == 1:
+        stage(T.m, T.s_m1)
+        call(xfer([c[2]], LOW, st, T.s_m1[:], S.m1))
+        call(xfer([c[0], c[3]], LOW, st, T.s_m1[:], S.m1), xfer([c[4]], HIGH, st, T.s_m1[:], S.m1))
+        carry(M4_PLAN[0], T.s_a4, S.a4)
+        sc.wait_ge(S.din, nt)
+        sc.dma_start(T.s_a4[:], T.d_in[:]).then_inc(S.ld3, 16)
+        make_u((S.a0, nl), (S.ld2, 16))
+        make_r((S.ld3, 16), (S.m5, nl))
+        make_q([(S.vv, nl)])
+        make_p(done("q"))
     elif r == 4:
         stage(T.mt, T.s_a4)
-        call(xfer([c[1]], THIN, st, T.d_m4[:], S.d4))
-        tail((S.ld2, 16), (S.m5, nl), (S.qt, nl))
+        call(*[xfer([x], THIN[k], st, T.d_in[:], S.din) for k, x in enumerate(carriers4) if k > 0])
+        call(xfer([carriers4[0]], THIN[0], st, T.d_in[:], S.din))
+        make_u((S.a0, nl), (S.m1, nh))
+        make_r((S.ld2, 16), (S.m5, nl))
+        make_q([(S.vv, nl)])
+        make_p(done("q"))
     else:
         stage(T.m, T.s_m5)
-        call(xfer([c[0]], LOW, st, T.s_m5[:], S.m5))
+        call(*[xfer([x], THIN[k], st, T.d_in[:], S.din) for k, x in enumerate(carriers5)])
+        call(xfer([c[0], c[3]], LOW, st, T.s_m5[:], S.m5))
         call(xfer([c[2]], HIGH, st, T.s_m5[:], S.m5))
-        tail((S.a4, nl), (S.ld2, 16), (S.qt, nl))
+        make_r((S.a4, nl), (S.ld2, 16))
+        make_p([(S.qt, nl)])
     g.wait_ge(S.snt, sent[0])

from concourse.bass import DstId, RemoteDMATransfer

M4_PLAN = [[2, 0], [5], [3]]
M5_PLAN = [[1], [4]]

_F = "float32"
_SB = ["s_a0", "s_m1", "s_a2", "s_m3", "s_a4", "s_m5", "s_ut", "s_v", "s_qt", "s_r", "s_p"]
SCRATCH = {
    "d_stage": ("dram", [128, 128], _F),
    "d_in": ("dram", [128, 128], _F),
}
for _n in _SB:
    SCRATCH[_n] = ("sbuf", [128, 128], _F)
for _k in range(8):
    SCRATCH["b%d" % _k] = ("psum", [128, 512], _F)

SEMAPHORES = ["ld", "ld2", "ld3", "a0", "m1", "a2", "m3", "din", "a4", "m5", "vv", "qt", "snt", "st"]
for _n in "vuqrp":
    for _k in range(2):
        SEMAPHORES += ["mm%s%d" % (_n, _k), "cp%s%d" % (_n, _k)]


def _engines(mask):
    return [b for b in range(mask.bit_length()) if (mask >> b) & 1]


def _as_mask(bits):
    m = 0
    for b in bits:
        m |= 1 << b
    return m


def _count(mask):
    return len(_engines(mask))


def rank_program(g, core, T, topo):
    r = T.rank_of(core)
    c = T.cores

    def outside(owner, target):
        return [x for x in range(topo.CORES_PER_CHIP * topo.CHIPS)
                if x not in c and topo.chip(x) == topo.chip(owner) and topo.die(x) == topo.die(owner)
                and topo.may_write(x, target)]

    carriers4 = [c[1]] + outside(c[4], c[3])[:len(M4_PLAN) - 1]
    carriers5 = outside(c[5], c[1])[:len(M5_PLAN)]
    if core not in c and core not in carriers4 and core not in carriers5:
        return
    S = T.sem
    te, ve, sy, sc = g.tensor, g.vector, g.sync, g.scalar

    near = [d for d in c if d != core and topo.chip(d) == topo.chip(core)]
    far = [d for d in c if topo.chip(d) != topo.chip(core)]
    on_eng = _engines(topo.mask(core, near[0]))
    off_eng = _engines(topo.mask(core, far[0]))
    LOW = _as_mask(off_eng)
    HIGH = _as_mask([e for e in on_eng if e not in off_eng])
    THIN = [_as_mask(on_eng[k::4]) for k in (0, 2, 1, 3)]
    nl, nh, nt = _count(LOW), _count(HIGH), _count(THIN[0])
    sent = [0]

    def xfer(dsts, mask, src, dst, sem):
        for d in dsts:
            if not topo.may_write(core, d) or (mask & ~topo.mask(core, d)):
                raise ValueError("core %d cannot write so to core %d" % (core, d))
        ids = [DstId(rid=topo.addr(d)[0], pnc=topo.addr(d)[1]) for d in dsts]
        sent[0] += _count(mask)
        return RemoteDMATransfer(dst_ids=ids, dma_engine_mask=mask, remote_sem=sem,
                                 srcs=[src], dsts=[dst for _ in dsts])

    def call(*transfers):
        g.remote_dma_fused(list(transfers), local_sem=S.snt)

    def product(name, lhsT, rhs, out, banks, ready, ready_half=None):
        for w in ready:
            te.wait_ge(*w)
        for h in range(2):
            cols = slice(64 * h, 64 * h + 64)
            if ready_half is not None:
                te.wait_ge(S["cp%s%d" % (ready_half, h)], 1)
            te.matmul(T[banks[h]][:, 0:64], lhsT[:], rhs[:, cols], True, True).then_inc(S["mm%s%d" % (name, h)], 1)
            ve.wait_ge(S["mm%s%d" % (name, h)], 1)
            ve.tensor_copy(out[:, cols], T[banks[h]][:, 0:64]).then_inc(S["cp%s%d" % (name, h)], 1)

    def done(name):
        return [(S["cp%s%d" % (name, h)], 1) for h in range(2)]

    def g_wait(waits):
        for w in waits:
            g.wait_ge(*w)

    def stage(inp, own=None):
        sy.dma_start(T.d_stage[:], inp[:]).then_inc(S.ld, 16)
        if own is not None:
            sc.wait_ge(S.ld, 16)
            sc.dma_start(own[:], inp[:]).then_inc(S.ld2, 16)
        g.wait_ge(S.ld, 16)

    def carry(ranks, dst, sem):
        g.wait_ge(S.din, nt)
        call(xfer([c[k] for k in ranks], LOW, T.d_in[:], dst[:], sem))

    def make_v(a2_ready, m3_ready):
        product("v", T.s_a2, T.s_m3, T.s_v, ("b0", "b7"), [a2_ready, m3_ready])

    def make_u(a0_ready, m1_ready):
        product("u", T.s_m1, T.s_a0, T.s_ut, ("b1", "b2"), [a0_ready, m1_ready])

    def make_q(v_ready):
        product("q", T.s_v, T.s_ut, T.s_qt, ("b3", "b4"), v_ready, "u")

    def make_r(a4_ready, m5_ready):
        product("r", T.s_a4, T.s_m5, T.s_r, ("b5", "b6"), [a4_ready, m5_ready])

    def make_p(qt_ready):
        product("p", T.s_qt, T.s_r, T.s_p, ("b0", "b7"), qt_ready, "r")
        for w in done("p"):
            sy.wait_ge(*w)
        sy.dma_start(T.y[:], T.s_p[:]).then_inc(S.st, 16)
        sy.wait_ge(S.st, 16)

    st = T.d_stage[:]
    if core in carriers5:
        carry(M5_PLAN[carriers5.index(core)], T.s_m5, S.m5)
    elif r is None:
        carry(M4_PLAN[carriers4.index(core)], T.s_a4, S.a4)
    elif r == 0:
        stage(T.mt, T.s_a0)
        call(xfer([c[2]], LOW, st, T.s_a0[:], S.a0))
        call(xfer([c[1], c[4]], LOW, st, T.s_a0[:], S.a0), xfer([c[3]], HIGH, st, T.s_a0[:], S.a0))
        g_wait(done("v"))
        call(xfer([c[1]], LOW, T.s_v[:], T.s_v[:], S.vv))
        make_v((S.a2, nl), (S.m3, nh))
        make_u((S.ld2, 16), (S.m1, nl))
        make_q(done("v"))
        make_r((S.a4, nl), (S.m5, nl))
        make_p(done("q"))
    elif r == 2:
        stage(T.mt, T.s_a2)
        call(xfer([c[0]], LOW, st, T.s_a2[:], S.a2))
        call(xfer([c[3]], LOW, st, T.s_a2[:], S.a2))
        g_wait(done("v"))
        call(xfer([c[4]], LOW, T.s_v[:], T.s_v[:], S.vv))
        g_wait(done("q"))
        call(xfer([c[5]], LOW, T.s_qt[:], T.s_qt[:], S.qt))
        make_v((S.ld2, 16), (S.m3, nl))
        make_u((S.a0, nl), (S.m1, nl))
        make_q(done("v"))
        make_r((S.a4, nl), (S.m5, nh))
        make_p(done("q"))
    elif r == 3:
        stage(T.m, T.s_m3)
        call(xfer([c[2]], LOW, st, T.s_m3[:], S.m3))
        call(xfer([c[0]], HIGH, st, T.s_m3[:], S.m3))
        make_v((S.a2, nl), (S.ld2, 16))
        make_u((S.a0, nh), (S.m1, nl))
        make_q(done("v"))
        make_r((S.a4, nl), (S.m5, nl))
        make_p(done("q"))
    elif r == 1:
        stage(T.m, T.s_m1)
        call(xfer([c[2]], LOW, st, T.s_m1[:], S.m1))
        call(xfer([c[0], c[3]], LOW, st, T.s_m1[:], S.m1), xfer([c[4]], HIGH, st, T.s_m1[:], S.m1))
        carry(M4_PLAN[0], T.s_a4, S.a4)
        sc.wait_ge(S.din, nt)
        sc.dma_start(T.s_a4[:], T.d_in[:]).then_inc(S.ld3, 16)
        make_u((S.a0, nl), (S.ld2, 16))
        make_r((S.ld3, 16), (S.m5, nl))
        make_q([(S.vv, nl)])
        make_p(done("q"))
    elif r == 4:
        stage(T.mt, T.s_a4)
        call(*[xfer([x], THIN[k], st, T.d_in[:], S.din) for k, x in enumerate(carriers4) if k > 0])
        call(xfer([carriers4[0]], THIN[0], st, T.d_in[:], S.din))
        make_u((S.a0, nl), (S.m1, nh))
        make_r((S.ld2, 16), (S.m5, nl))
        make_q([(S.vv, nl)])
        make_p(done("q"))
    else:
        stage(T.m, T.s_m5)
        call(*[xfer([x], THIN[k], st, T.d_in[:], S.din) for k, x in enumerate(carriers5)])
        call(xfer([c[0], c[3]], LOW, st, T.s_m5[:], S.m5))
        call(xfer([c[2]], HIGH, st, T.s_m5[:], S.m5))
        make_r((S.a4, nl), (S.ld2, 16))
        make_p([(S.qt, nl)])
    g.wait_ge(S.snt, sent[0])
